import numpy as np
import ml_dtypes


def mxq(x, axis, fmt="e4m3"):
    dtype, down = {"e4m3": (ml_dtypes.float8_e4m3fn, 7), "e5m2": (ml_dtypes.float8_e5m2, 14)}[fmt]
    v = np.moveaxis(np.asarray(x, np.float32).astype(ml_dtypes.bfloat16).astype(np.float64), axis, -1)
    blocks = v.reshape(v.shape[:-1] + (-1, 32))
    amax = np.abs(blocks).max(-1, keepdims=True)
    byte = np.maximum(np.where(amax > 0, np.frexp(amax)[1] - 1 + 127, 0) - down, 1)
    scale = np.exp2(byte - 127.0)
    codes = (blocks / scale).astype(np.float32).astype(dtype).astype(np.float64)
    return np.moveaxis((codes * scale).reshape(v.shape), -1, axis)


WIDE = False


def mx_kscale(k):
    if not WIDE:
        return np.ones(k)
    levels = np.array([10, -10, 5, -5, 0])
    if k % 512:
        return np.exp2(np.random.permutation(np.resize(levels, k // 32))).repeat(32)
    a = np.empty((k // 512, 16))
    for p in range(k // 512):
        a[p, :8] = np.random.permutation(np.resize(levels, 8))
        for g in range(8):
            far = levels[np.abs(levels - a[p, g]) >= 10]
            a[p, g + 8] = far[np.random.randint(len(far))]
    return np.exp2(a.ravel()).repeat(32)


BF16 = ml_dtypes.bfloat16


def bf(x):
    return np.asarray(x, np.float32).astype(BF16)


def f64(x):
    return np.asarray(x).astype(np.float64)


E2M1 = np.array([0.0, 0.5, 1.0, 1.5, 2.0, 3.0, 4.0, 6.0, -0.0, -0.5, -1.0, -1.5, -2.0, -3.0, -4.0, -6.0])


def pack_weight(w, fmt):
    k, n = w.shape
    w = f64(bf(w)).reshape(k // 32, 32, n)
    amax = np.abs(w).max(1)
    if fmt == "e4m3":
        byte = np.frexp(amax)[1] - 1 + 127 - 7
    else:
        mant, ex = np.frexp(amax / 6.0)
        byte = np.where(mant > 0.5, ex, ex - 1) + 127
    byte = np.clip(np.where(amax > 0, byte, 1), 1, 254)
    scaled = (w * np.exp2(127.0 - byte)[:, None, :]).reshape(k, n).astype(np.float32)
    by_word = np.ascontiguousarray(scaled.reshape(k // 512, 128, 4, n).transpose(0, 1, 3, 2))
    if fmt == "e4m3":
        words = by_word.astype(ml_dtypes.float8_e4m3fn).view(np.uint8)
    else:
        c = by_word.astype(ml_dtypes.float4_e2m1fn).view(np.uint8) & 0xF
        words = c[..., 0::2] | (c[..., 1::2] << 4)
    return np.ascontiguousarray(words), np.ascontiguousarray(byte.astype(np.uint8).reshape(k // 512, 16, n))


def unpack_weight(words, scales, fmt):
    g, p, n, _ = words.shape
    if fmt == "e4m3":
        vals = np.ascontiguousarray(words).view(ml_dtypes.float8_e4m3fn).astype(np.float64)
    else:
        nib = np.empty((g, p, n, 4), np.uint8)
        nib[..., 0::2] = words & 0xF
        nib[..., 1::2] = words >> 4
        vals = E2M1[nib]
    vals = vals * np.repeat(np.exp2(scales.astype(np.float64) - 127.0), 8, axis=1)[..., None]
    return vals.transpose(0, 1, 3, 2).reshape(g * 512, n)
def pack4(w):
    words, scales = pack_weight(w, "e2m1")
    return words.reshape(words.shape[0], 128, -1), scales


def unpack4(words, scales):
    return unpack_weight(words.reshape(words.shape[0], 128, -1, 2), scales, "e2m1")


M, N, E, D, HK, H, HV = 512, 1024, 1024, 1024, 8, 4, 2


def draw0():
    s = mx_kscale(E)
    r = mx_kscale(E)
    t = mx_kscale(D)
    x = np.random.standard_normal((M, E)) * s
    wq = np.random.standard_normal((E, D)) / np.sqrt(E) / s[:, None] * t
    y = np.random.standard_normal((N, E)) * r
    wk = np.random.standard_normal((E, D)) / np.sqrt(E) / r[:, None] / t
    wk_words, wk_scales = pack4(wk)
    return {"x": bf(x), "wq": bf(wq), "y": bf(y),
            "wk_words": wk_words, "wk_scales": wk_scales,
            "pl": bf(np.random.standard_normal((H, HK)) / np.sqrt(D)),
            "pw": bf(np.random.standard_normal((H, HV)) / np.sqrt(H))}


def core(x, wq, y, wk_words, wk_scales, pl, pw):
    qry = mxq(f64(x), 1, "e4m3") @ mxq(f64(wq), 0, "e4m3")
    key = mxq(f64(y), 1, "e4m3") @ unpack4(wk_words, wk_scales)
    z = (qry.reshape(M, HK, D // HK) * f64(pl)[:, None, :, None]).reshape(H * M, D)
    logits = mxq(z, 1, "e4m3") @ mxq(key, 1, "e4m3").T
    att = np.maximum(logits, 0.0).reshape(H, M, N)
    return (att[:, None] * f64(pw)[:, :, None, None]).sum(axis=0)


def e4m3fn_bytes(y):
    return np.clip(np.asarray(y, np.float64), -448.0, 448.0).astype(np.float32).astype(ml_dtypes.float8_e4m3fn).view(np.uint8)


def e4m3fn_values(b):
    return np.asarray(b, np.uint8).view(ml_dtypes.float8_e4m3fn).astype(np.float64)


def setup_inputs():
    d = draw0()
    x0 = np.asarray(d['y']).astype(np.float64)
    s = (np.max(np.abs(x0), axis=(0,), keepdims=True) / 448.0).astype(np.float32)
    out = {}
    for k, v in d.items():
        if k == 'y':
            out['y_bytes'] = e4m3fn_bytes(x0 / s.astype(np.float64))
            out['y_scale'] = s
        else:
            out[k] = v
    return out


def reference(x, wq, y_bytes, y_scale, wk_words, wk_scales, pl, pw):
    return core(x, wq, e4m3fn_values(y_bytes) * y_scale.astype(np.float64), wk_words, wk_scales, pl, pw)

@@ -1,0 +1,514 @@
+from contextlib import ExitStack
+
+import concourse.mybir as mybir
+from concourse.masks import make_identity
+
+M, N, E, D, HK, H, HV = 512, 1024, 1024, 1024, 8, 4, 2
+FLOPS = 2 * M * E * D + 2 * N * E * D + 2 * H * M * N * D
+
+F32 = mybir.dt.float32
+BF16 = mybir.dt.bfloat16
+I32 = mybir.dt.int32
+U32 = mybir.dt.uint32
+U8 = mybir.dt.uint8
+FP8 = mybir.dt.float8_e4m3fn
+FP8X4 = mybir.dt.float8_e4m3fn_x4
+FP4X4 = mybir.dt.float4_e2m1fn_x4
+MULT = mybir.AluOpType.mult
+ADD = mybir.AluOpType.add
+MAX = mybir.AluOpType.max
+RELU = mybir.ActivationFunctionType.Relu
+COPY = mybir.ActivationFunctionType.Copy
+
+P = 128
+MIXED = (3,)
+F = {
+    ("lay", 0): 0,
+    ("lay", 1): 2,
+    ("lay", 2): 3,
+    ("lay", 3): 4,
+    ("first", 0, 0, 0): True,
+    ("first", 0, 0, 1): False,
+    ("first", 1, 0, 0): True,
+    ("first", 1, 0, 1): False,
+    ("first", 2, 0, 0): True,
+    ("first", 2, 0, 1): False,
+    ("relu", 0, 0): True,
+    ("relu", 0, 1): True,
+    ("relu", 0, 2): True,
+    ("relu", 0, 3): True,
+    ("mixout", 0, 0): True,
+    ("mixout", 0, 1): True,
+    ("first", 0, 1, 0): True,
+    ("first", 0, 1, 1): False,
+    ("first", 1, 1, 0): True,
+    ("first", 1, 1, 1): False,
+    ("first", 2, 1, 0): True,
+    ("first", 2, 1, 1): False,
+    ("relu", 1, 0): True,
+    ("relu", 1, 1): True,
+    ("relu", 1, 2): True,
+    ("relu", 1, 3): True,
+    ("mixout", 1, 0): True,
+    ("mixout", 1, 1): True,
+    ("key", 0, 0): True,
+    ("key", 0, 1): True,
+    ("key", 1, 0): True,
+    ("key", 1, 1): True,
+    ("key", 2, 0): True,
+    ("key", 2, 1): True,
+    ("key", 3, 0): True,
+    ("key", 3, 1): True,
+    ("key", 4, 0): True,
+    ("key", 4, 1): True,
+    ("key", 5, 0): True,
+    ("key", 5, 1): True,
+    ("key", 6, 0): True,
+    ("key", 6, 1): True,
+    ("key", 7, 0): True,
+    ("key", 7, 1): True,
+    ("q", 0, 0): True,
+    ("zs", 0, 0): 0,
+    ("q", 0, 1): True,
+    ("zs", 0, 1): 1,
+    ("q", 1, 0): True,
+    ("zs", 1, 0): 0,
+    ("q", 1, 1): True,
+    ("zs", 1, 1): 1,
+    ("q", 2, 0): True,
+    ("zs", 2, 0): 0,
+    ("q", 2, 1): True,
+    ("zs", 2, 1): 1,
+    ("q", 3, 0): True,
+    ("zs", 3, 0): 0,
+    ("q", 3, 1): True,
+    ("zs", 3, 1): 1,
+    ("bc", 0): False,
+    ("bc", 1): True,
+}
+
+
+def tile_talking_heads_relu_map_s11_kernel(
+    tc, x, wq, y_bytes, y_scale, wk_words, wk_scales, pl, pw, out
+):
+    nc = tc.nc
+    with ExitStack() as ctx:
+        keep = ctx.enter_context(tc.tile_pool(name="keep", bufs=1))
+        work = ctx.enter_context(tc.tile_pool(name="work", bufs=3))
+        psum = ctx.enter_context(tc.psum_pool(name="psum", bufs=8))
+        ctx.enter_context(tc.manual_schedule())
+
+        x_sb = keep.tile([P, 4, E], BF16, align_bytes=64)
+        wq_raw = keep.tile([P, 4, 4, 512], BF16, align_bytes=64)
+        yb_sb = keep.tile([P, 8, E], U8, align_bytes=64)
+        ysc = keep.tile([P, E], F32, align_bytes=64)
+        ysv = keep.tile([P, 2, 4], F32, align_bytes=64)
+        wkw_raw = keep.tile([P, 2, 2048], U8, align_bytes=64)
+        wks_raw = keep.tile([P, 2, 1024], U8, align_bytes=64)
+        wkw = keep.tile([P, 4096], U8, align_bytes=64)
+        wks = keep.tile([P, 2048], U8, align_bytes=64)
+        plb = keep.tile([P, H * HK], BF16, align_bytes=64)
+        pwb = keep.tile([P, H * HV], BF16, align_bytes=64)
+
+        nc.scalar.dma_start(out=plb[:], in_=pl.rearrange("h i -> (h i)").partition_broadcast(P))
+        nc.scalar.dma_start(out=pwb[:], in_=pw.rearrange("h v -> (h v)").partition_broadcast(P))
+        nc.vector.memset(wks_raw[:].bitcast(I32), 0)
+
+        def load_y(a):
+            nc.sync.dma_start(
+                out=yb_sb[:, a : a + 2, :],
+                in_=y_bytes[a * P : (a + 2) * P, :].rearrange("(a p) k -> p a k", p=P),
+            )
+
+        def load_wq(e, g):
+            nc.sync.dma_start(
+                out=wq_raw[:, 2 * g + e],
+                in_=wq[512 * e : 512 * (e + 1), 512 * g : 512 * (g + 1)].rearrange("(p j) d -> p j d", j=4),
+            )
+
+        def load_x(mt):
+            nc.sync.dma_start(out=x_sb[:, mt], in_=x[P * mt : P * (mt + 1), :])
+
+        def load_wk():
+            nc.sync.dma_start(out=wkw_raw[:], in_=wk_words.rearrange("e p b -> p e b"))
+            for q in range(4):
+                nc.sync.dma_start(
+                    out=wks_raw[32 * q : 32 * q + 4].bitcast(I32),
+                    in_=wk_scales.bitcast(I32)[:, 4 * q : 4 * q + 4, :].rearrange("e s n -> s e n"),
+                )
+
+        L = {"s": lambda: nc.sync.dma_start(out=ysv[:], in_=y_scale.rearrange("o (b p m) -> p (o b) m", b=2, m=4)), "k": load_wk}
+        for c in range(4): L["w%d" % c] = lambda c=c: load_wq(c % 2, c // 2)
+        for a in range(0, 8, 2): L["y%d" % a] = lambda a=a: load_y(a)
+        for a in range(4): L["x%d" % a] = lambda a=a: load_x(a)
+        for name in "s y6 y0 y4 x3 x2 y2 w0 x1 w1 w2 x0 k w3".split():
+            L[name]()
+
+        ident = keep.tile([P, P], F32)
+        make_identity(nc, ident[:])
+        plf = keep.tile([P, H, 2], F32)
+        pwf = keep.tile([P, H * HV], F32)
+        pwp = keep.tile([P, HV], F32)
+        nc.gpsimd.tensor_copy(out=pwf[:], in_=pwb[:])
+        for q in range(4):
+            rows = slice(32 * q, 32 * q + 32)
+            nc.gpsimd.tensor_copy(
+                out=plf[rows], in_=plb[rows].rearrange("p (h g q) -> p h g q", h=H, g=2)[:, :, :, q]
+            )
+            nc.gpsimd.tensor_copy(out=pwp[rows], in_=pwb[rows, 2 * q : 2 * q + 2])
+        fold = keep.tile([P, 32], F32)
+        wmix = keep.tile([P, 2, P], F32)
+        nc.gpsimd.tensor_tensor(out=fold[:], in0=ident[:, 0:32], in1=ident[:, 32:64], op=ADD)
+        nc.gpsimd.tensor_tensor(out=fold[:], in0=fold[:], in1=ident[:, 64:96], op=ADD)
+        nc.gpsimd.tensor_tensor(out=fold[:], in0=fold[:], in1=ident[:, 96:128], op=ADD)
+        nc.gpsimd.memset(wmix[:], 0.0)
+        for j in range(2):
+            for v in range(HV):
+                c0 = 64 * v + 32 * j
+                nc.gpsimd.tensor_scalar(
+                    out=wmix[:, j, c0 : c0 + 32], in0=fold[:], scalar1=pwp[:, v : v + 1], scalar2=None, op0=MULT
+                )
+
+        xc = keep.tile([P, 4, 256], U32, align_bytes=64)
+        xs = keep.tile([P, 4, 256], U8, align_bytes=64)
+        yc = keep.tile([P, 8, 256], U32, align_bytes=64)
+        ys = keep.tile([P, 8, 256], U8, align_bytes=64)
+        wqc = keep.tile([P, 4, 512], U32, align_bytes=64)
+        wqs = keep.tile([P, 4, 512], U8, align_bytes=64)
+        kc = keep.tile([P, 4, 512], U32, align_bytes=64)
+        ks = keep.tile([P, 4, 512], U8, align_bytes=64)
+        zc = keep.tile([P, 8, 512], U32, align_bytes=64)
+        zs = keep.tile([P, 8, 512], U8, align_bytes=64)
+
+        def bank(nm):
+            return psum.tile([P, 512], F32, tag="bank", name=nm)
+
+        def turn(src, nm):
+            words = src.bitcast(F32)
+            tr = bank("tr" + nm)
+            for gu in range(4):
+                g, u = gu // 2, gu % 2
+                nc.tensor.transpose(
+                    tr[:, P * gu : P * (gu + 1)], words[:, 256 * g + u : 256 * (g + 1) : 2], ident[:]
+                )
+            return tr
+
+        def turned(tr, dst):
+            nc.scalar.copy(
+                out=dst.bitcast(F32).rearrange("p (g r u) -> p g r u", g=2, u=2),
+                in_=tr[:].rearrange("p (g u r) -> p g r u", g=2, u=2),
+            )
+
+        def x_item(mt):
+            s = {}
+
+            def mm():
+                s["tr"] = turn(x_sb[:, mt, :], "x%d" % mt)
+
+            def leave():
+                s["xg"] = work.tile([P, E], BF16, align_bytes=64, tag="xg", name="xg_%d" % mt, bufs=2)
+                turned(s["tr"], s["xg"][:])
+
+            def fin():
+                nc.vector.quantize_mx(out=xc[:, mt].bitcast(FP8X4), scales=xs[:, mt], in_=s["xg"][:])
+
+            return (None, mm, leave, fin, None)
+
+        def y_item(nt):
+            s = {}
+
+            def prep():
+                s["yw"] = work.tile([P, E], BF16, align_bytes=64, tag="yw", name="yw_%d" % nt)
+                nc.vector.tensor_tensor(out=s["yw"][:], in0=yb_sb[:, nt, :].bitcast(FP8), in1=ysc[:], op=MULT)
+
+            def mm():
+                s["tr"] = turn(s["yw"][:], "y%d" % nt)
+
+            def leave():
+                s["yg"] = work.tile([P, E], BF16, align_bytes=64, tag="yg", name="yg_%d" % nt, bufs=5)
+                turned(s["tr"], s["yg"][:])
+
+            def fin():
+                nc.vector.quantize_mx(out=yc[:, nt].bitcast(FP8X4), scales=ys[:, nt], in_=s["yg"][:])
+
+            return (prep, mm, leave, fin, None)
+
+        def wq_item(c):
+            s = {}
+
+            def prep():
+                s["wg"] = work.tile([P, 2048], BF16, align_bytes=64, tag="wg", name="wg_%d" % c)
+                src = wq_raw[:, c].rearrange("p j (q t i) -> p t q j i", t=4, i=4)
+                dst = s["wg"][:].rearrange("p (t q i j) -> p t q j i", t=4, i=4, j=4)
+                nv = F["lay", c]
+                if nv:
+                    nc.vector.tensor_copy(out=dst[:, 0:nv], in_=src[:, 0:nv])
+                for t in range(nv, 4):
+                    nc.scalar.copy(out=dst[:, t], in_=src[:, t])
+
+            def fin():
+                nc.vector.quantize_mx(out=wqc[:, c].bitcast(FP8X4), scales=wqs[:, c], in_=s["wg"][:])
+
+            return (prep, None, None, fin, None)
+
+        def scale_item():
+            s = {}
+
+            def mm():
+                for b in range(2):
+                    s[b] = bank("bc%d" % b)
+                    for m in range(4):
+                        nc.tensor.transpose(
+                            s[b][:, P * m : P * (m + 1)],
+                            ysv[:, b, m : m + 1].to_broadcast([P, P]),
+                            ident[:],
+                        )
+
+            def leave():
+                for b in range(2):
+                    (nc.scalar.copy if F["bc", b] else nc.vector.tensor_copy)(
+                        out=ysc[:, 512 * b : 512 * (b + 1)].rearrange("p (i m) -> p i m", m=4),
+                        in_=s[b][:].rearrange("p (m i) -> p i m", m=4),
+                    )
+
+            return (None, mm, leave, None, None)
+
+        def wk_item():
+            def prep():
+                nc.vector.tensor_copy(
+                    out=wkw[:].bitcast(I32).rearrange("p (t x r) -> p t x r", t=4, r=2),
+                    in_=wkw_raw[:].rearrange("p e b -> p (e b)").bitcast(I32).rearrange("p (x t r) -> p t x r", t=4, r=2),
+                )
+                nc.vector.tensor_copy(
+                    out=wks[:].bitcast(I32).rearrange("p (t x) -> p t x", t=4),
+                    in_=wks_raw[:].rearrange("p e b -> p (e b)").bitcast(I32).rearrange("p (x t) -> p t x", t=4),
+                )
+
+            return (prep, None, None, None, None)
+
+        kgs = {}
+
+        def key_item(nt, g):
+            s = {}
+            nh, a = nt // 4, nt % 4
+
+            def mm():
+                s["kp"] = bank("kp%d%d" % (nt, g))
+                for t in range(4):
+                    for e in range(2):
+                        col = ((2 * t + e) * 2 + g) * P
+                        nc.tensor.matmul_mx(
+                            out=s["kp"][:, P * t : P * (t + 1)],
+                            lhsT=wkw[:, 2 * col : 2 * col + 256].bitcast(FP4X4),
+                            lhsT_scale=wks[:, col : col + P],
+                            rhs=yc[:, nt, P * e : P * (e + 1)].bitcast(FP8X4),
+                            rhs_scale=ys[:, nt, P * e : P * (e + 1)],
+                            start=(e == 0),
+                            stop=(e == 1),
+                        )
+
+            def leave():
+                if a == 0:
+                    kgs[nh, g] = work.tile([P, 4, 512], BF16, align_bytes=64, tag="kg", name="kg_%d%d" % (nh, g), bufs=4)
+                (nc.scalar.copy if F["key", nt, g] else nc.vector.tensor_copy)(
+                    out=kgs[nh, g][:, a, :].rearrange("p (n t) -> p n t", t=4),
+                    in_=s["kp"][:].rearrange("p (t n) -> p n t", t=4),
+                )
+
+            def fin():
+                nc.vector.quantize_mx(
+                    out=kc[:, 2 * nh + g].bitcast(FP8X4),
+                    scales=ks[:, 2 * nh + g],
+                    in_=kgs[nh, g][:].rearrange("p a c -> p (a c)"),
+                )
+
+            return (None, mm, leave, fin if a == 3 else None, None)
+
+        def z_item(mt, g):
+            s = {}
+
+            def mm():
+                s["qp"] = bank("qp%d%d" % (mt, g))
+                for t in range(4):
+                    for e in range(2):
+                        nc.tensor.matmul_mx(
+                            out=s["qp"][:, P * t : P * (t + 1)],
+                            lhsT=wqc[:, 2 * g + e, P * t : P * (t + 1)].bitcast(FP8X4),
+                            lhsT_scale=wqs[:, 2 * g + e, P * t : P * (t + 1)],
+                            rhs=xc[:, mt, P * e : P * (e + 1)].bitcast(FP8X4),
+                            rhs_scale=xs[:, mt, P * e : P * (e + 1)],
+                            start=(e == 0),
+                            stop=(e == 1),
+                        )
+
+            def leave():
+                s["qf"] = work.tile([P, 512], F32, align_bytes=64, tag="qf", name="qf_%d%d" % (mt, g))
+                src = s["qp"][:].rearrange("p (t m) -> p m t", t=4)
+                (nc.scalar.copy if F["q", mt, g] else nc.vector.tensor_copy)(
+                    out=s["qf"][:].rearrange("p (m t) -> p m t", t=4), in_=src
+                )
+                s["zb"] = work.tile([P, 2048], BF16, align_bytes=64, tag="zb", name="zb_%d%d" % (mt, g), bufs=4)
+                for h in range(F["zs", mt, g]):
+                    nc.scalar.activation(out=zdst(s["zb"], h, "p (b m t) -> p b m t"), in_=src if mt not in MIXED else src.rearrange("p (b m) t -> p b m t", b=4), func=COPY, scale=plf[:, h, g : g + 1])
+
+            def zdst(zb, h, pat):
+                if mt in MIXED:
+                    return zb[:].rearrange("p (b h m t) -> p b h m t", b=4, h=H, t=4)[:, :, h]
+                return zb[:, 512 * h : 512 * (h + 1)].rearrange("p (m t) -> p m t", t=4)
+
+            def fin():
+                zb = s["zb"]
+                for h in range(F["zs", mt, g], H):
+                    if mt in MIXED:
+                        dst = zb[:].rearrange("p (b h c) -> p b h c", b=4, h=H)[:, :, h, :]
+                        src = s["qf"][:].rearrange("p (b c) -> p b c", b=4)
+                    else:
+                        dst = zb[:, 512 * h : 512 * (h + 1)]
+                        src = s["qf"][:]
+                    nc.vector.tensor_scalar(out=dst, in0=src, scalar1=plf[:, h, g : g + 1], scalar2=None, op0=MULT)
+
+            def late():
+                nc.vector.quantize_mx(out=zc[:, 2 * mt + g].bitcast(FP8X4), scales=zs[:, 2 * mt + g], in_=s["zb"][:])
+
+            return (None, mm, leave, fin, late)
+
+        def logits(mt, nh, b):
+            lp = bank("lp%d%d%d" % (mt, nh, b))
+            for g in range(2):
+                nc.tensor.matmul_mx(
+                    out=lp[:],
+                    lhsT=zc[:, 2 * mt + g, P * b : P * (b + 1)].bitcast(FP8X4),
+                    lhsT_scale=zs[:, 2 * mt + g, P * b : P * (b + 1)],
+                    rhs=kc[:, 2 * nh + g].bitcast(FP8X4),
+                    rhs_scale=ks[:, 2 * nh + g],
+                    start=(g == 0),
+                    stop=(g == 1),
+                )
+            return lp
+
+        accs = {}
+
+        def direct_item(mt, nh, h):
+            s = {}
+
+            def mm():
+                s["lp"] = logits(mt, nh, h)
+
+            def leave():
+                s["att"] = work.tile([P, 512], F32, tag="att", name="att%d%d%d" % (mt, nh, h), bufs=8)
+                nc.scalar.activation(out=s["att"][:], in_=s["lp"][:], func=RELU)
+                if h == 0:
+                    for v in range(HV):
+                        accs[mt, nh, v] = work.tile([P, 512], F32, tag="acc%d" % v, name="acc%d%d%d" % (mt, nh, v), bufs=3)
+                        if F["first", mt, nh, v]:
+                            nc.scalar.activation(out=accs[mt, nh, v][:], in_=s["att"][:], func=COPY, scale=pwf[:, v : v + 1])
+
+            def fin():
+                for v in range(HV):
+                    w = pwf[:, 2 * h + v : 2 * h + v + 1]
+                    acc = accs[mt, nh, v]
+                    if h > 0:
+                        nc.vector.scalar_tensor_tensor(
+                            out=acc[:], in0=s["att"][:], scalar=w, in1=acc[:], op0=MULT, op1=ADD
+                        )
+                    elif not F["first", mt, nh, v]:
+                        nc.vector.tensor_scalar(out=acc[:], in0=s["att"][:], scalar1=w, scalar2=None, op0=MULT)
+                    if h == H - 1:
+                        nc.sync.dma_start(
+                            out=out[v, P * mt : P * (mt + 1), 512 * nh : 512 * (nh + 1)], in_=acc[:]
+                        )
+
+            return (None, mm, leave, fin, None)
+
+        atts = {}
+
+        def relu_item(mt, nh, b):
+            s = {}
+
+            def mm():
+                s["lp"] = logits(mt, nh, b)
+
+            def leave():
+                atts[nh, b] = work.tile([P, 512], F32, tag="rel", name="att%d%d%d" % (mt, nh, b), bufs=4)
+                if F["relu", nh, b]:
+                    nc.scalar.activation(out=atts[nh, b][:], in_=s["lp"][:], func=RELU)
+                else:
+                    nc.vector.tensor_scalar(out=atts[nh, b][:], in0=s["lp"][:], scalar1=0.0, scalar2=None, op0=MAX)
+
+            return (None, mm, leave, None, None)
+
+        def mix_item(mt, nh, pair):
+            s = {}
+
+            def mm():
+                s["mix"] = bank("mix%d%d" % (nh, pair))
+                for j in range(2):
+                    nc.tensor.matmul(
+                        s["mix"][:], lhsT=wmix[:, j, :], rhs=atts[nh, 2 * pair + j][:], start=(j == 0), stop=(j == 1)
+                    )
+
+            def leave():
+                res = work.tile([P, 512], F32, tag="res", name="res%d%d" % (nh, pair), bufs=2)
+                if F["mixout", nh, pair]:
+                    nc.scalar.copy(out=res[:], in_=s["mix"][:])
+                else:
+                    nc.vector.tensor_copy(out=res[:], in_=s["mix"][:])
+                r0 = P * mt + 64 * pair
+                for v in range(HV):
+                    nc.sync.dma_start(
+                        out=out[v, r0 : r0 + 64, 512 * nh : 512 * (nh + 1)], in_=res[64 * v : 64 * (v + 1), :]
+                    )
+
+            return (None, mm, leave, None, None)
+
+        def direct(mt, nh):
+            return [direct_item(mt, nh, h) for h in range(H)]
+
+        def mixed(mt, nh):
+            r = [relu_item(mt, nh, b) for b in range(4)]
+            m = [mix_item(mt, nh, pair) for pair in range(2)]
+            return [r[0], r[1], r[2], m[0], r[3], (None, None, None, None), m[1]]
+
+        def weave(main, side):
+            out_list = []
+            for i, item in enumerate(main):
+                out_list.append(item)
+                out_list.extend(side[i * len(side) // len(main) : (i + 1) * len(side) // len(main)])
+            return out_list
+
+        def zs_of(mt):
+            return [z_item(mt, g) for g in range(2)]
+
+        def keys_of(nh):
+            return [key_item(4 * nh + a, g) for g in range(2) for a in range(4)]
+
+        items = {}
+        for c in range(4): items["w%d" % c] = wq_item(c)
+        for a in range(8): items["y%d" % a] = y_item(a)
+        for a in range(4): items["x%d" % a] = x_item(a)
+        items["K"] = wk_item()
+        for a in range(8):
+            for g in range(2): items["k%d%d" % (a, g)] = key_item(a, g)
+        for a in range(4):
+            for g in range(2): items["z%d%d" % (a, g)] = z_item(a, g)
+        for nh in range(2):
+            for mt in range(3):
+                for h in range(4): items["l%d%d%d" % (mt, nh, h)] = direct_item(mt, nh, h)
+            for b in range(4): items["l3%d%d" % (nh, b)] = relu_item(3, nh, b)
+            for b in range(2): items["m%d%d" % (nh, b)] = mix_item(3, nh, b)
+        items["b"] = scale_item()
+        order = (
+            "b y6 y0 x3 x1 y1 y3 y5 y2 w0 y4 w1 y7 x2 "
+            "K w3 w2 x0 k00 k10 k20 k30 k01 z30 k11 k21 z31 k31 "
+            "k40 z10 k50 k60 z11 k70 k41 z00 k51 k61 z01 k71 z20 z21 "
+            "l100 l101 l102 l300 l103 l010 l301 l011 l302 l012 l013 m00 l000 l303 "
+            "l001 l002 m01 l003 l310 l210 l211 l311 l212 l312 l213 l200 m10 l201 "
+            "l313 l202 l203 m11 l110 l111 l112 l113 "
+        ).split()
+        lags = {"w": (0, 1, 4, 6, 6), "y": (0, 2, 6, 7, 12), "x": (0, 1, 6, 11, 12), "k": (0, 0, 1, 8, 13), "z": (0, 4, 5, 9, 11), "l": (0, 4, 8, 9, 10), "m": (0, 8, 12, 12, 12), "K": (0, 4, 7, 8, 10), "b": (0, 0, 1, 3, 10)}
+        last = max(max(v) for v in lags.values())
+        for step in range(len(order) + last):
+            for stage in (4, 3, 2, 1, 0):
+                for i, key in enumerate(order):
+                    if i + lags[key[0]][stage] == step and items[key][stage] is not None:
+                        items[key][stage]()

@@ -16,75 +16,37 @@ FP8X4 = mybir.dt.float8_e4m3fn_x4
 FP4X4 = mybir.dt.float4_e2m1fn_x4
 MULT = mybir.AluOpType.mult
 ADD = mybir.AluOpType.add
-MAX = mybir.AluOpType.max
 RELU = mybir.ActivationFunctionType.Relu
 COPY = mybir.ActivationFunctionType.Copy
 
 P = 128
-MIXED = (3,)
-F = {
-    ("lay", 0): 0,
-    ("lay", 1): 2,
-    ("lay", 2): 3,
-    ("lay", 3): 4,
-    ("first", 0, 0, 0): True,
-    ("first", 0, 0, 1): False,
-    ("first", 1, 0, 0): True,
-    ("first", 1, 0, 1): False,
-    ("first", 2, 0, 0): True,
-    ("first", 2, 0, 1): False,
-    ("relu", 0, 0): True,
-    ("relu", 0, 1): True,
-    ("relu", 0, 2): True,
-    ("relu", 0, 3): True,
-    ("mixout", 0, 0): True,
-    ("mixout", 0, 1): True,
-    ("first", 0, 1, 0): True,
-    ("first", 0, 1, 1): False,
-    ("first", 1, 1, 0): True,
-    ("first", 1, 1, 1): False,
-    ("first", 2, 1, 0): True,
-    ("first", 2, 1, 1): False,
-    ("relu", 1, 0): True,
-    ("relu", 1, 1): True,
-    ("relu", 1, 2): True,
-    ("relu", 1, 3): True,
-    ("mixout", 1, 0): True,
-    ("mixout", 1, 1): True,
-    ("key", 0, 0): True,
-    ("key", 0, 1): True,
-    ("key", 1, 0): True,
-    ("key", 1, 1): True,
-    ("key", 2, 0): True,
-    ("key", 2, 1): True,
-    ("key", 3, 0): True,
-    ("key", 3, 1): True,
-    ("key", 4, 0): True,
-    ("key", 4, 1): True,
-    ("key", 5, 0): True,
-    ("key", 5, 1): True,
-    ("key", 6, 0): True,
-    ("key", 6, 1): True,
-    ("key", 7, 0): True,
-    ("key", 7, 1): True,
-    ("q", 0, 0): True,
-    ("zs", 0, 0): 0,
-    ("q", 0, 1): True,
-    ("zs", 0, 1): 1,
-    ("q", 1, 0): True,
-    ("zs", 1, 0): 0,
-    ("q", 1, 1): True,
-    ("zs", 1, 1): 1,
-    ("q", 2, 0): True,
-    ("zs", 2, 0): 0,
-    ("q", 2, 1): True,
-    ("zs", 2, 1): 1,
-    ("q", 3, 0): True,
-    ("zs", 3, 0): 0,
-    ("q", 3, 1): True,
-    ("zs", 3, 1): 1,
-    ("bc", 0): False,
-    ("bc", 1): True,
+PASS = 512
+BANK = 512
+MIXED = 3
+
+WQ_PLANES_ON_VECTOR = (1, 0, 4, 2)
+HEADS_ON_SCALAR = (1, 1, 0, 0, 0, 2, 0, 1)
+MAPS_ON_SCALAR = (0, 0, 0, 1, 1, 1)
+
+LOADS = "scale y0 heads x1 x3 y2 w1 x2 y4 x0 wk_scales y6 w0 wk w3 w2".split()
+INPUT_ITEMS = "scale y1 x1 x3 heads y0 y3 w1 y2 x2 y5 x0 y4 y7 y6 wk w0 w3 w2".split()
+KEY_HALVES = (0, 1)
+QUERY_TILES = (1, 3, 0, 2)
+GROUPS = ((1, 0), (0, 0), (2, 1), (0, 1), (2, 0), (1, 1))
+QUERIES_AMONG_KEYS = (5, 1)
+MIXED_AMONG_MAPS = (3, 1.5)
+LAGS = {
+    "scale": (0, 0, 1, 5, 5),
+    "heads": (0, 1, 3, 3, 5),
+    "w": (0, 4, 10, 10, 10),
+    "y": (0, 3, 4, 8, 13),
+    "x": (0, 0, 1, 8, 13),
+    "wk": (0, 4, 5, 11, 13),
+    "key": (0, 0, 3, 9, 9),
+    "query": (0, 4, 5, 7, 10),
+    "map": (0, 0, 2, 7, 7),
+    "relu": (0, 0, 2, 7, 7),
+    "mix": (0, 3, 5, 5, 11),
 }
 
 
@@ -99,416 +61,433 @@ def tile_talking_heads_relu_map_s11_kernel(
         ctx.enter_context(tc.manual_schedule())
 
         x_sb = keep.tile([P, 4, E], BF16, align_bytes=64)
-        wq_raw = keep.tile([P, 4, 4, 512], BF16, align_bytes=64)
-        yb_sb = keep.tile([P, 8, E], U8, align_bytes=64)
-        ysc = keep.tile([P, E], F32, align_bytes=64)
-        ysv = keep.tile([P, 2, 4], F32, align_bytes=64)
-        wkw_raw = keep.tile([P, 2, 2048], U8, align_bytes=64)
-        wks_raw = keep.tile([P, 2, 1024], U8, align_bytes=64)
-        wkw = keep.tile([P, 4096], U8, align_bytes=64)
-        wks = keep.tile([P, 2048], U8, align_bytes=64)
-        plb = keep.tile([P, H * HK], BF16, align_bytes=64)
-        pwb = keep.tile([P, H * HV], BF16, align_bytes=64)
+        wq_raw = keep.tile([P, 4, 4, PASS], BF16, align_bytes=64)
+        y_codes = keep.tile([P, 8, E], U8, align_bytes=64)
+        scale_rows = keep.tile([P, E], F32, align_bytes=64)
+        scale_cols = keep.tile([P, 2, 4], F32, align_bytes=64)
+        wk_words_raw = keep.tile([P, 2, 2 * D], U8, align_bytes=64)
+        wk_scales_raw = keep.tile([P, 2, D], U8, align_bytes=64)
+        wk_w = keep.tile([P, 4 * D], U8, align_bytes=64)
+        wk_s = keep.tile([P, 2 * D], U8, align_bytes=64)
+        heads_row = keep.tile([P, H * HK + H * HV], BF16, align_bytes=64)
 
-        nc.scalar.dma_start(out=plb[:], in_=pl.rearrange("h i -> (h i)").partition_broadcast(P))
-        nc.scalar.dma_start(out=pwb[:], in_=pw.rearrange("h v -> (h v)").partition_broadcast(P))
-        nc.vector.memset(wks_raw[:].bitcast(I32), 0)
+        nc.vector.memset(heads_row[:], 0.0)
+        nc.vector.memset(wk_scales_raw[:].bitcast(I32), 0)
 
         def load_y(a):
-            nc.sync.dma_start(
-                out=yb_sb[:, a : a + 2, :],
-                in_=y_bytes[a * P : (a + 2) * P, :].rearrange("(a p) k -> p a k", p=P),
-            )
+            rows = y_bytes[a * P : (a + 2) * P, :]
+            nc.sync.dma_start(out=y_codes[:, a : a + 2, :], in_=rows.rearrange("(a p) k -> p a k", p=P))
 
-        def load_wq(e, g):
-            nc.sync.dma_start(
-                out=wq_raw[:, 2 * g + e],
-                in_=wq[512 * e : 512 * (e + 1), 512 * g : 512 * (g + 1)].rearrange("(p j) d -> p j d", j=4),
-            )
+        def load_wq(c):
+            g, e = c // 2, c % 2
+            block = wq[PASS * e : PASS * (e + 1), PASS * g : PASS * (g + 1)]
+            nc.sync.dma_start(out=wq_raw[:, c], in_=block.rearrange("(p j) d -> p j d", j=4))
 
         def load_x(mt):
             nc.sync.dma_start(out=x_sb[:, mt], in_=x[P * mt : P * (mt + 1), :])
 
         def load_wk():
-            nc.sync.dma_start(out=wkw_raw[:], in_=wk_words.rearrange("e p b -> p e b"))
+            nc.sync.dma_start(out=wk_words_raw[:], in_=wk_words.rearrange("e p b -> p e b"))
+
+        def load_wk_scales():
             for q in range(4):
                 nc.sync.dma_start(
-                    out=wks_raw[32 * q : 32 * q + 4].bitcast(I32),
+                    out=wk_scales_raw[32 * q : 32 * q + 4].bitcast(I32),
                     in_=wk_scales.bitcast(I32)[:, 4 * q : 4 * q + 4, :].rearrange("e s n -> s e n"),
                 )
 
-        L = {"s": lambda: nc.sync.dma_start(out=ysv[:], in_=y_scale.rearrange("o (b p m) -> p (o b) m", b=2, m=4)), "k": load_wk}
-        for c in range(4): L["w%d" % c] = lambda c=c: load_wq(c % 2, c // 2)
-        for a in range(0, 8, 2): L["y%d" % a] = lambda a=a: load_y(a)
-        for a in range(4): L["x%d" % a] = lambda a=a: load_x(a)
-        for name in "s y6 y0 y4 x3 x2 y2 w0 x1 w1 w2 x0 k w3".split():
-            L[name]()
+        def load_scale():
+            nc.sync.dma_start(out=scale_cols[:], in_=y_scale.rearrange("o (b p m) -> p (o b) m", b=2, m=4))
+
+        def load_heads():
+            nc.sync.dma_start(out=heads_row[0:1, 0 : H * HK], in_=pl.rearrange("(o h) i -> o (h i)", o=1))
+            nc.sync.dma_start(out=heads_row[0:1, H * HK :], in_=pw.rearrange("(o h) v -> o (h v)", o=1))
+
+        loads = {"scale": load_scale, "heads": load_heads, "wk": load_wk, "wk_scales": load_wk_scales}
+        for a in range(4):
+            loads["w%d" % a] = lambda c=a: load_wq(c)
+            loads["x%d" % a] = lambda mt=a: load_x(mt)
+            loads["y%d" % (2 * a)] = lambda nt=2 * a: load_y(nt)
+        for name in LOADS:
+            loads[name]()
 
         ident = keep.tile([P, P], F32)
         make_identity(nc, ident[:])
-        plf = keep.tile([P, H, 2], F32)
-        pwf = keep.tile([P, H * HV], F32)
-        pwp = keep.tile([P, HV], F32)
-        nc.gpsimd.tensor_copy(out=pwf[:], in_=pwb[:])
-        for q in range(4):
-            rows = slice(32 * q, 32 * q + 32)
-            nc.gpsimd.tensor_copy(
-                out=plf[rows], in_=plb[rows].rearrange("p (h g q) -> p h g q", h=H, g=2)[:, :, :, q]
-            )
-            nc.gpsimd.tensor_copy(out=pwp[rows], in_=pwb[rows, 2 * q : 2 * q + 2])
+        ones = keep.tile([P, P], BF16)
+        nc.gpsimd.memset(ones[:], 1.0)
+        pl_col = keep.tile([P, H, 2], F32)
+        pw_row = keep.tile([P, H * HV], F32)
+        pw_col = keep.tile([P, HV], F32)
         fold = keep.tile([P, 32], F32)
-        wmix = keep.tile([P, 2, P], F32)
+        mixer = keep.tile([P, 2, P], F32)
         nc.gpsimd.tensor_tensor(out=fold[:], in0=ident[:, 0:32], in1=ident[:, 32:64], op=ADD)
         nc.gpsimd.tensor_tensor(out=fold[:], in0=fold[:], in1=ident[:, 64:96], op=ADD)
         nc.gpsimd.tensor_tensor(out=fold[:], in0=fold[:], in1=ident[:, 96:128], op=ADD)
-        nc.gpsimd.memset(wmix[:], 0.0)
-        for j in range(2):
-            for v in range(HV):
-                c0 = 64 * v + 32 * j
-                nc.gpsimd.tensor_scalar(
-                    out=wmix[:, j, c0 : c0 + 32], in0=fold[:], scalar1=pwp[:, v : v + 1], scalar2=None, op0=MULT
-                )
+        nc.gpsimd.memset(mixer[:], 0.0)
 
-        xc = keep.tile([P, 4, 256], U32, align_bytes=64)
-        xs = keep.tile([P, 4, 256], U8, align_bytes=64)
-        yc = keep.tile([P, 8, 256], U32, align_bytes=64)
-        ys = keep.tile([P, 8, 256], U8, align_bytes=64)
-        wqc = keep.tile([P, 4, 512], U32, align_bytes=64)
-        wqs = keep.tile([P, 4, 512], U8, align_bytes=64)
-        kc = keep.tile([P, 4, 512], U32, align_bytes=64)
-        ks = keep.tile([P, 4, 512], U8, align_bytes=64)
-        zc = keep.tile([P, 8, 512], U32, align_bytes=64)
-        zs = keep.tile([P, 8, 512], U8, align_bytes=64)
+        x_c = keep.tile([P, 4, 256], U32, align_bytes=64)
+        x_s = keep.tile([P, 4, 256], U8, align_bytes=64)
+        y_c = keep.tile([P, 8, 256], U32, align_bytes=64)
+        y_s = keep.tile([P, 8, 256], U8, align_bytes=64)
+        wq_c = keep.tile([P, 4, PASS], U32, align_bytes=64)
+        wq_s = keep.tile([P, 4, PASS], U8, align_bytes=64)
+        key_c = keep.tile([P, 4, BANK], U32, align_bytes=64)
+        key_s = keep.tile([P, 4, BANK], U8, align_bytes=64)
+        z_c = keep.tile([P, 8, H * P], U32, align_bytes=64)
+        z_s = keep.tile([P, 8, H * P], U8, align_bytes=64)
 
-        def bank(nm):
-            return psum.tile([P, 512], F32, tag="bank", name=nm)
+        def bank(name):
+            return psum.tile([P, BANK], F32, tag="bank", name=name)
 
-        def turn(src, nm):
+        def scale_item():
+            s = {}
+
+            def tensor():
+                for b in range(2):
+                    s[b] = bank("scale%d" % b)
+                    for m in range(4):
+                        column = scale_cols[:, b, m : m + 1].to_broadcast([P, P])
+                        nc.tensor.transpose(s[b][:, P * m : P * (m + 1)], column, ident[:])
+
+            def empty():
+                for b in range(2):
+                    row = scale_rows[:, PASS * b : PASS * (b + 1)]
+                    nc.scalar.copy(
+                        out=row.rearrange("p (i m) -> p i m", m=4), in_=s[b][:].rearrange("p (m i) -> p i m", m=4)
+                    )
+
+            return (None, tensor, empty, None, None)
+
+        def heads_item():
+            s = {}
+
+            def tensor():
+                s["all"] = bank("heads")
+                nc.tensor.matmul(s["all"][:, 0 : H * HK + H * HV], lhsT=ones[:], rhs=heads_row[:], start=True, stop=True)
+
+            def empty():
+                pl_all = s["all"][:, 0 : H * HK].rearrange("p (h g q) -> p h g q", h=H, g=2)
+                pw_all = s["all"][:, H * HK : H * HK + H * HV]
+                nc.scalar.copy(out=pw_row[:], in_=pw_all)
+                for q in range(4):
+                    rows = slice(32 * q, 32 * q + 32)
+                    nc.scalar.copy(out=pl_col[rows], in_=pl_all[rows, :, :, q])
+                    nc.scalar.copy(out=pw_col[rows], in_=pw_all[rows, HV * q : HV * (q + 1)])
+                for j in range(2):
+                    for v in range(HV):
+                        cols = slice(64 * v + 32 * j, 64 * v + 32 * j + 32)
+                        nc.gpsimd.tensor_scalar(
+                            out=mixer[:, j, cols], in0=fold[:], scalar1=pw_col[:, v : v + 1], scalar2=None, op0=MULT
+                        )
+
+            return (None, tensor, empty, None, None)
+
+        def wq_item(c):
+            s = {}
+
+            def prepare():
+                s["grouped"] = work.tile([P, 4 * PASS], BF16, align_bytes=64, tag="wq", name="wq_%d" % c)
+                dst = s["grouped"][:].rearrange("p (t q r j) -> p t q r j", t=4, r=8, j=4)
+                src = wq_raw[:, c].rearrange("p j (q t r) -> p t q r j", t=4, r=8)
+                on_vector = WQ_PLANES_ON_VECTOR[c]
+                if on_vector:
+                    nc.vector.tensor_copy(out=dst[:, 0:on_vector], in_=src[:, 0:on_vector])
+                for t in range(on_vector, 4):
+                    nc.scalar.copy(out=dst[:, t], in_=src[:, t])
+
+            def finish():
+                nc.vector.quantize_mx(out=wq_c[:, c].bitcast(FP8X4), scales=wq_s[:, c], in_=s["grouped"][:])
+
+            return (prepare, None, None, finish, None)
+
+        def turn(src, name):
             words = src.bitcast(F32)
-            tr = bank("tr" + nm)
-            for gu in range(4):
-                g, u = gu // 2, gu % 2
-                nc.tensor.transpose(
-                    tr[:, P * gu : P * (gu + 1)], words[:, 256 * g + u : 256 * (g + 1) : 2], ident[:]
-                )
-            return tr
+            turned = bank(name)
+            for e in range(2):
+                for u in range(2):
+                    c0 = P * (2 * e + u)
+                    nc.tensor.transpose(turned[:, c0 : c0 + P], words[:, 256 * e + u : 256 * (e + 1) : 2], ident[:])
+            return turned
 
-        def turned(tr, dst):
+        def empty_turned(turned, dst):
             nc.scalar.copy(
-                out=dst.bitcast(F32).rearrange("p (g r u) -> p g r u", g=2, u=2),
-                in_=tr[:].rearrange("p (g u r) -> p g r u", g=2, u=2),
+                out=dst.bitcast(F32).rearrange("p (e r u) -> p e r u", e=2, u=2),
+                in_=turned[:].rearrange("p (e u r) -> p e r u", e=2, u=2),
             )
 
         def x_item(mt):
             s = {}
 
-            def mm():
-                s["tr"] = turn(x_sb[:, mt, :], "x%d" % mt)
+            def tensor():
+                s["turned"] = turn(x_sb[:, mt, :], "turn_x%d" % mt)
 
-            def leave():
-                s["xg"] = work.tile([P, E], BF16, align_bytes=64, tag="xg", name="xg_%d" % mt, bufs=2)
-                turned(s["tr"], s["xg"][:])
+            def empty():
+                s["grouped"] = work.tile([P, E], BF16, align_bytes=64, tag="x", name="x_%d" % mt, bufs=2)
+                empty_turned(s["turned"], s["grouped"][:])
 
-            def fin():
-                nc.vector.quantize_mx(out=xc[:, mt].bitcast(FP8X4), scales=xs[:, mt], in_=s["xg"][:])
+            def finish():
+                nc.vector.quantize_mx(out=x_c[:, mt].bitcast(FP8X4), scales=x_s[:, mt], in_=s["grouped"][:])
 
-            return (None, mm, leave, fin, None)
+            return (None, tensor, empty, finish, None)
 
         def y_item(nt):
             s = {}
 
-            def prep():
-                s["yw"] = work.tile([P, E], BF16, align_bytes=64, tag="yw", name="yw_%d" % nt)
-                nc.vector.tensor_tensor(out=s["yw"][:], in0=yb_sb[:, nt, :].bitcast(FP8), in1=ysc[:], op=MULT)
-
-            def mm():
-                s["tr"] = turn(s["yw"][:], "y%d" % nt)
-
-            def leave():
-                s["yg"] = work.tile([P, E], BF16, align_bytes=64, tag="yg", name="yg_%d" % nt, bufs=5)
-                turned(s["tr"], s["yg"][:])
-
-            def fin():
-                nc.vector.quantize_mx(out=yc[:, nt].bitcast(FP8X4), scales=ys[:, nt], in_=s["yg"][:])
-
-            return (prep, mm, leave, fin, None)
-
-        def wq_item(c):
-            s = {}
-
-            def prep():
-                s["wg"] = work.tile([P, 2048], BF16, align_bytes=64, tag="wg", name="wg_%d" % c)
-                src = wq_raw[:, c].rearrange("p j (q t i) -> p t q j i", t=4, i=4)
-                dst = s["wg"][:].rearrange("p (t q i j) -> p t q j i", t=4, i=4, j=4)
-                nv = F["lay", c]
-                if nv:
-                    nc.vector.tensor_copy(out=dst[:, 0:nv], in_=src[:, 0:nv])
-                for t in range(nv, 4):
-                    nc.scalar.copy(out=dst[:, t], in_=src[:, t])
-
-            def fin():
-                nc.vector.quantize_mx(out=wqc[:, c].bitcast(FP8X4), scales=wqs[:, c], in_=s["wg"][:])
-
-            return (prep, None, None, fin, None)
-
-        def scale_item():
-            s = {}
-
-            def mm():
+            def prepare():
+                s["rows"] = work.tile([P, E], BF16, align_bytes=64, tag="y_rows", name="y_rows_%d" % nt)
                 for b in range(2):
-                    s[b] = bank("bc%d" % b)
-                    for m in range(4):
-                        nc.tensor.transpose(
-                            s[b][:, P * m : P * (m + 1)],
-                            ysv[:, b, m : m + 1].to_broadcast([P, P]),
-                            ident[:],
-                        )
-
-            def leave():
-                for b in range(2):
-                    (nc.scalar.copy if F["bc", b] else nc.vector.tensor_copy)(
-                        out=ysc[:, 512 * b : 512 * (b + 1)].rearrange("p (i m) -> p i m", m=4),
-                        in_=s[b][:].rearrange("p (m i) -> p i m", m=4),
+                    cols = slice(PASS * b, PASS * (b + 1))
+                    nc.vector.tensor_tensor(
+                        out=s["rows"][:, cols],
+                        in0=y_codes[:, nt, cols].bitcast(FP8),
+                        in1=scale_rows[:, cols],
+                        op=MULT,
                     )
 
-            return (None, mm, leave, None, None)
+            def tensor():
+                s["turned"] = turn(s["rows"][:], "turn_y%d" % nt)
+
+            def empty():
+                s["grouped"] = work.tile([P, E], BF16, align_bytes=64, tag="y", name="y_%d" % nt, bufs=5)
+                empty_turned(s["turned"], s["grouped"][:])
+
+            def finish():
+                nc.vector.quantize_mx(out=y_c[:, nt].bitcast(FP8X4), scales=y_s[:, nt], in_=s["grouped"][:])
+
+            return (prepare, tensor, empty, finish, None)
 
         def wk_item():
-            def prep():
-                nc.vector.tensor_copy(
-                    out=wkw[:].bitcast(I32).rearrange("p (t x r) -> p t x r", t=4, r=2),
-                    in_=wkw_raw[:].rearrange("p e b -> p (e b)").bitcast(I32).rearrange("p (x t r) -> p t x r", t=4, r=2),
-                )
-                nc.vector.tensor_copy(
-                    out=wks[:].bitcast(I32).rearrange("p (t x) -> p t x", t=4),
-                    in_=wks_raw[:].rearrange("p e b -> p (e b)").bitcast(I32).rearrange("p (x t) -> p t x", t=4),
-                )
+            def prepare():
+                for dst, src, run in ((wk_w, wk_words_raw, 4), (wk_s, wk_scales_raw, 2)):
+                    nc.vector.tensor_copy(
+                        out=dst[:].bitcast(I32).rearrange("p (t x r) -> p t x r", t=4, r=run),
+                        in_=src[:].rearrange("p e b -> p (e b)").bitcast(I32).rearrange("p (x t r) -> p t x r", t=4, r=run),
+                    )
 
-            return (prep, None, None, None, None)
+            return (prepare, None, None, None, None)
 
-        kgs = {}
+        key_grouped = {}
 
         def key_item(nt, g):
             s = {}
-            nh, a = nt // 4, nt % 4
+            half, a = nt // 4, nt % 4
 
-            def mm():
-                s["kp"] = bank("kp%d%d" % (nt, g))
+            def tensor():
+                s["key"] = bank("key%d%d" % (nt, g))
                 for t in range(4):
                     for e in range(2):
-                        col = ((2 * t + e) * 2 + g) * P
+                        col = P * ((2 * t + e) * 2 + g)
                         nc.tensor.matmul_mx(
-                            out=s["kp"][:, P * t : P * (t + 1)],
-                            lhsT=wkw[:, 2 * col : 2 * col + 256].bitcast(FP4X4),
-                            lhsT_scale=wks[:, col : col + P],
-                            rhs=yc[:, nt, P * e : P * (e + 1)].bitcast(FP8X4),
-                            rhs_scale=ys[:, nt, P * e : P * (e + 1)],
+                            out=s["key"][:, P * t : P * (t + 1)],
+                            lhsT=wk_w[:, 2 * col : 2 * (col + P)].bitcast(FP4X4),
+                            lhsT_scale=wk_s[:, col : col + P],
+                            rhs=y_c[:, nt, P * e : P * (e + 1)].bitcast(FP8X4),
+                            rhs_scale=y_s[:, nt, P * e : P * (e + 1)],
                             start=(e == 0),
                             stop=(e == 1),
                         )
 
-            def leave():
+            def empty():
                 if a == 0:
-                    kgs[nh, g] = work.tile([P, 4, 512], BF16, align_bytes=64, tag="kg", name="kg_%d%d" % (nh, g), bufs=4)
-                (nc.scalar.copy if F["key", nt, g] else nc.vector.tensor_copy)(
-                    out=kgs[nh, g][:, a, :].rearrange("p (n t) -> p n t", t=4),
-                    in_=s["kp"][:].rearrange("p (t n) -> p n t", t=4),
+                    key_grouped[half, g] = work.tile(
+                        [P, 4, 4 * P], BF16, align_bytes=64, tag="key", name="key_%d%d" % (half, g), bufs=4
+                    )
+                nc.scalar.copy(
+                    out=key_grouped[half, g][:, a, :].rearrange("p (n t) -> p n t", t=4),
+                    in_=s["key"][:].rearrange("p (t n) -> p n t", t=4),
                 )
 
-            def fin():
+            def finish():
                 nc.vector.quantize_mx(
-                    out=kc[:, 2 * nh + g].bitcast(FP8X4),
-                    scales=ks[:, 2 * nh + g],
-                    in_=kgs[nh, g][:].rearrange("p a c -> p (a c)"),
+                    out=key_c[:, 2 * half + g].bitcast(FP8X4),
+                    scales=key_s[:, 2 * half + g],
+                    in_=key_grouped[half, g][:].rearrange("p a c -> p (a c)"),
                 )
 
-            return (None, mm, leave, fin if a == 3 else None, None)
+            return (None, tensor, empty, finish if a == 3 else None, None)
 
-        def z_item(mt, g):
+        def z_columns(z, mt):
+            if mt == MIXED:
+                return z.rearrange("p (b h c) -> p h b c", b=4, h=H)
+            return z.rearrange("p (h b c) -> p h b c", h=H, b=1)
+
+        def query_item(mt, g):
             s = {}
 
-            def mm():
-                s["qp"] = bank("qp%d%d" % (mt, g))
+            def tensor():
+                s["query"] = bank("query%d%d" % (mt, g))
                 for t in range(4):
                     for e in range(2):
+                        c = 2 * g + e
                         nc.tensor.matmul_mx(
-                            out=s["qp"][:, P * t : P * (t + 1)],
-                            lhsT=wqc[:, 2 * g + e, P * t : P * (t + 1)].bitcast(FP8X4),
-                            lhsT_scale=wqs[:, 2 * g + e, P * t : P * (t + 1)],
-                            rhs=xc[:, mt, P * e : P * (e + 1)].bitcast(FP8X4),
-                            rhs_scale=xs[:, mt, P * e : P * (e + 1)],
+                            out=s["query"][:, P * t : P * (t + 1)],
+                            lhsT=wq_c[:, c, P * t : P * (t + 1)].bitcast(FP8X4),
+                            lhsT_scale=wq_s[:, c, P * t : P * (t + 1)],
+                            rhs=x_c[:, mt, P * e : P * (e + 1)].bitcast(FP8X4),
+                            rhs_scale=x_s[:, mt, P * e : P * (e + 1)],
                             start=(e == 0),
                             stop=(e == 1),
                         )
 
-            def leave():
-                s["qf"] = work.tile([P, 512], F32, align_bytes=64, tag="qf", name="qf_%d%d" % (mt, g))
-                src = s["qp"][:].rearrange("p (t m) -> p m t", t=4)
-                (nc.scalar.copy if F["q", mt, g] else nc.vector.tensor_copy)(
-                    out=s["qf"][:].rearrange("p (m t) -> p m t", t=4), in_=src
-                )
-                s["zb"] = work.tile([P, 2048], BF16, align_bytes=64, tag="zb", name="zb_%d%d" % (mt, g), bufs=4)
-                for h in range(F["zs", mt, g]):
-                    nc.scalar.activation(out=zdst(s["zb"], h, "p (b m t) -> p b m t"), in_=src if mt not in MIXED else src.rearrange("p (b m) t -> p b m t", b=4), func=COPY, scale=plf[:, h, g : g + 1])
+            def empty():
+                s["float"] = work.tile([P, BANK], F32, align_bytes=64, tag="query", name="query_%d%d" % (mt, g))
+                by_token = s["query"][:].rearrange("p (t m) -> p m t", t=4)
+                nc.scalar.copy(out=s["float"][:].rearrange("p (m t) -> p m t", t=4), in_=by_token)
+                s["z"] = work.tile([P, H * BANK], BF16, align_bytes=64, tag="z", name="z_%d%d" % (mt, g), bufs=4)
+                for h in range(HEADS_ON_SCALAR[2 * mt + g]):
+                    dst = z_columns(s["z"][:], mt)[:, h].rearrange("p b (m t) -> p b m t", t=4)
+                    nc.scalar.activation(
+                        out=dst,
+                        in_=by_token.rearrange("p (b m) t -> p b m t", b=dst.shape[1]),
+                        func=COPY,
+                        scale=pl_col[:, h, g : g + 1],
+                    )
 
-            def zdst(zb, h, pat):
-                if mt in MIXED:
-                    return zb[:].rearrange("p (b h m t) -> p b h m t", b=4, h=H, t=4)[:, :, h]
-                return zb[:, 512 * h : 512 * (h + 1)].rearrange("p (m t) -> p m t", t=4)
+            def finish():
+                for h in range(HEADS_ON_SCALAR[2 * mt + g], H):
+                    dst = z_columns(s["z"][:], mt)[:, h]
+                    nc.vector.tensor_scalar(
+                        out=dst,
+                        in0=s["float"][:].rearrange("p (b c) -> p b c", b=dst.shape[1]),
+                        scalar1=pl_col[:, h, g : g + 1],
+                        scalar2=None,
+                        op0=MULT,
+                    )
 
-            def fin():
-                zb = s["zb"]
-                for h in range(F["zs", mt, g], H):
-                    if mt in MIXED:
-                        dst = zb[:].rearrange("p (b h c) -> p b h c", b=4, h=H)[:, :, h, :]
-                        src = s["qf"][:].rearrange("p (b c) -> p b c", b=4)
-                    else:
-                        dst = zb[:, 512 * h : 512 * (h + 1)]
-                        src = s["qf"][:]
-                    nc.vector.tensor_scalar(out=dst, in0=src, scalar1=plf[:, h, g : g + 1], scalar2=None, op0=MULT)
+            def finish_further():
+                nc.vector.quantize_mx(out=z_c[:, 2 * mt + g].bitcast(FP8X4), scales=z_s[:, 2 * mt + g], in_=s["z"][:])
 
-            def late():
-                nc.vector.quantize_mx(out=zc[:, 2 * mt + g].bitcast(FP8X4), scales=zs[:, 2 * mt + g], in_=s["zb"][:])
+            return (None, tensor, empty, finish, finish_further)
 
-            return (None, mm, leave, fin, late)
-
-        def logits(mt, nh, b):
-            lp = bank("lp%d%d%d" % (mt, nh, b))
+        def logits(mt, half, block):
+            result = bank("logits%d%d%d" % (mt, half, block))
+            cols = slice(P * block, P * (block + 1))
             for g in range(2):
                 nc.tensor.matmul_mx(
-                    out=lp[:],
-                    lhsT=zc[:, 2 * mt + g, P * b : P * (b + 1)].bitcast(FP8X4),
-                    lhsT_scale=zs[:, 2 * mt + g, P * b : P * (b + 1)],
-                    rhs=kc[:, 2 * nh + g].bitcast(FP8X4),
-                    rhs_scale=ks[:, 2 * nh + g],
+                    out=result[:],
+                    lhsT=z_c[:, 2 * mt + g, cols].bitcast(FP8X4),
+                    lhsT_scale=z_s[:, 2 * mt + g, cols],
+                    rhs=key_c[:, 2 * half + g].bitcast(FP8X4),
+                    rhs_scale=key_s[:, 2 * half + g],
                     start=(g == 0),
                     stop=(g == 1),
                 )
-            return lp
+            return result
 
-        accs = {}
+        sums = {}
 
-        def direct_item(mt, nh, h):
+        def map_item(mt, half, h):
             s = {}
+            on_scalar = MAPS_ON_SCALAR[3 * half + mt]
 
-            def mm():
-                s["lp"] = logits(mt, nh, h)
+            def tensor():
+                s["logits"] = logits(mt, half, h)
 
-            def leave():
-                s["att"] = work.tile([P, 512], F32, tag="att", name="att%d%d%d" % (mt, nh, h), bufs=8)
-                nc.scalar.activation(out=s["att"][:], in_=s["lp"][:], func=RELU)
+            def empty():
+                s["att"] = work.tile([P, BANK], F32, tag="att", name="att%d%d%d" % (mt, half, h), bufs=8)
+                nc.scalar.activation(out=s["att"][:], in_=s["logits"][:], func=RELU)
                 if h == 0:
                     for v in range(HV):
-                        accs[mt, nh, v] = work.tile([P, 512], F32, tag="acc%d" % v, name="acc%d%d%d" % (mt, nh, v), bufs=3)
-                        if F["first", mt, nh, v]:
-                            nc.scalar.activation(out=accs[mt, nh, v][:], in_=s["att"][:], func=COPY, scale=pwf[:, v : v + 1])
+                        sums[mt, half, v] = work.tile(
+                            [P, BANK], F32, tag="sum%d" % v, name="sum%d%d%d" % (mt, half, v), bufs=3
+                        )
+                        if v < on_scalar:
+                            nc.scalar.activation(
+                                out=sums[mt, half, v][:], in_=s["att"][:], func=COPY, scale=pw_row[:, v : v + 1]
+                            )
 
-            def fin():
+            def finish():
                 for v in range(HV):
-                    w = pwf[:, 2 * h + v : 2 * h + v + 1]
-                    acc = accs[mt, nh, v]
+                    weight = pw_row[:, HV * h + v : HV * h + v + 1]
+                    total = sums[mt, half, v]
                     if h > 0:
                         nc.vector.scalar_tensor_tensor(
-                            out=acc[:], in0=s["att"][:], scalar=w, in1=acc[:], op0=MULT, op1=ADD
+                            out=total[:], in0=s["att"][:], scalar=weight, in1=total[:], op0=MULT, op1=ADD
                         )
-                    elif not F["first", mt, nh, v]:
-                        nc.vector.tensor_scalar(out=acc[:], in0=s["att"][:], scalar1=w, scalar2=None, op0=MULT)
+                    elif v >= on_scalar:
+                        nc.vector.tensor_scalar(out=total[:], in0=s["att"][:], scalar1=weight, scalar2=None, op0=MULT)
                     if h == H - 1:
                         nc.sync.dma_start(
-                            out=out[v, P * mt : P * (mt + 1), 512 * nh : 512 * (nh + 1)], in_=acc[:]
+                            out=out[v, P * mt : P * (mt + 1), BANK * half : BANK * (half + 1)], in_=total[:]
                         )
 
-            return (None, mm, leave, fin, None)
+            return (None, tensor, empty, finish, None)
 
         atts = {}
 
-        def relu_item(mt, nh, b):
+        def relu_item(half, block):
             s = {}
 
-            def mm():
-                s["lp"] = logits(mt, nh, b)
+            def tensor():
+                s["logits"] = logits(MIXED, half, block)
 
-            def leave():
-                atts[nh, b] = work.tile([P, 512], F32, tag="rel", name="att%d%d%d" % (mt, nh, b), bufs=4)
-                if F["relu", nh, b]:
-                    nc.scalar.activation(out=atts[nh, b][:], in_=s["lp"][:], func=RELU)
-                else:
-                    nc.vector.tensor_scalar(out=atts[nh, b][:], in0=s["lp"][:], scalar1=0.0, scalar2=None, op0=MAX)
+            def empty():
+                atts[half, block] = work.tile([P, BANK], F32, tag="relu", name="relu%d%d" % (half, block), bufs=4)
+                nc.scalar.activation(out=atts[half, block][:], in_=s["logits"][:], func=RELU)
 
-            return (None, mm, leave, None, None)
+            return (None, tensor, empty, None, None)
 
-        def mix_item(mt, nh, pair):
+        def mix_item(half, pair):
             s = {}
 
-            def mm():
-                s["mix"] = bank("mix%d%d" % (nh, pair))
+            def tensor():
+                s["mix"] = bank("mix%d%d" % (half, pair))
                 for j in range(2):
                     nc.tensor.matmul(
-                        s["mix"][:], lhsT=wmix[:, j, :], rhs=atts[nh, 2 * pair + j][:], start=(j == 0), stop=(j == 1)
+                        s["mix"][:],
+                        lhsT=mixer[:, j, :],
+                        rhs=atts[half, 2 * pair + j][:],
+                        start=(j == 0),
+                        stop=(j == 1),
                     )
 
-            def leave():
-                res = work.tile([P, 512], F32, tag="res", name="res%d%d" % (nh, pair), bufs=2)
-                if F["mixout", nh, pair]:
-                    nc.scalar.copy(out=res[:], in_=s["mix"][:])
-                else:
-                    nc.vector.tensor_copy(out=res[:], in_=s["mix"][:])
-                r0 = P * mt + 64 * pair
+            def empty():
+                res = work.tile([P, BANK], F32, tag="res", name="res%d%d" % (half, pair), bufs=2)
+                nc.scalar.copy(out=res[:], in_=s["mix"][:])
+                m0 = P * MIXED + 64 * pair
                 for v in range(HV):
                     nc.sync.dma_start(
-                        out=out[v, r0 : r0 + 64, 512 * nh : 512 * (nh + 1)], in_=res[64 * v : 64 * (v + 1), :]
+                        out=out[v, m0 : m0 + 64, BANK * half : BANK * (half + 1)], in_=res[64 * v : 64 * (v + 1), :]
                     )
 
-            return (None, mm, leave, None, None)
+            return (None, tensor, empty, None, None)
 
-        def direct(mt, nh):
-            return [direct_item(mt, nh, h) for h in range(H)]
+        items = []
+        for name in INPUT_ITEMS:
+            if name == "scale":
+                items.append((name, scale_item()))
+            elif name == "heads":
+                items.append((name, heads_item()))
+            elif name == "wk":
+                items.append((name, wk_item()))
+            else:
+                kind, number = name[0], int(name[1])
+                items.append((kind, {"w": wq_item, "y": y_item, "x": x_item}[kind](number)))
 
-        def mixed(mt, nh):
-            r = [relu_item(mt, nh, b) for b in range(4)]
-            m = [mix_item(mt, nh, pair) for pair in range(2)]
-            return [r[0], r[1], r[2], m[0], r[3], (None, None, None, None), m[1]]
+        keys = [("key", key_item(4 * half + a, g)) for half in KEY_HALVES for g in range(2) for a in range(4)]
+        queries = [("query", query_item(mt, g)) for mt in QUERY_TILES for g in range(2)]
+        maps = [("map", map_item(mt, half, h)) for mt, half in GROUPS for h in range(H)]
+        mixed = []
+        for half in range(2):
+            relus = [("relu", relu_item(half, block)) for block in range(4)]
+            mixes = [("mix", mix_item(half, pair)) for pair in range(2)]
+            mixed += relus[0:3] + mixes[0:1] + relus[3:4] + mixes[1:2]
 
-        def weave(main, side):
-            out_list = []
+        def weave(main, side, first, every):
+            woven, taken = [], 0
             for i, item in enumerate(main):
-                out_list.append(item)
-                out_list.extend(side[i * len(side) // len(main) : (i + 1) * len(side) // len(main)])
-            return out_list
+                woven.append(item)
+                while taken < len(side) and i >= first + every * taken:
+                    woven.append(side[taken])
+                    taken += 1
+            return woven + side[taken:]
 
-        def zs_of(mt):
-            return [z_item(mt, g) for g in range(2)]
+        items += weave(keys, queries, *QUERIES_AMONG_KEYS)
+        items += weave(maps, mixed, *MIXED_AMONG_MAPS)
 
-        def keys_of(nh):
-            return [key_item(4 * nh + a, g) for g in range(2) for a in range(4)]
-
-        items = {}
-        for c in range(4): items["w%d" % c] = wq_item(c)
-        for a in range(8): items["y%d" % a] = y_item(a)
-        for a in range(4): items["x%d" % a] = x_item(a)
-        items["K"] = wk_item()
-        for a in range(8):
-            for g in range(2): items["k%d%d" % (a, g)] = key_item(a, g)
-        for a in range(4):
-            for g in range(2): items["z%d%d" % (a, g)] = z_item(a, g)
-        for nh in range(2):
-            for mt in range(3):
-                for h in range(4): items["l%d%d%d" % (mt, nh, h)] = direct_item(mt, nh, h)
-            for b in range(4): items["l3%d%d" % (nh, b)] = relu_item(3, nh, b)
-            for b in range(2): items["m%d%d" % (nh, b)] = mix_item(3, nh, b)
-        items["b"] = scale_item()
-        order = (
-            "b y6 y0 x3 x1 y1 y3 y5 y2 w0 y4 w1 y7 x2 "
-            "K w3 w2 x0 k00 k10 k20 k30 k01 z30 k11 k21 z31 k31 "
-            "k40 z10 k50 k60 z11 k70 k41 z00 k51 k61 z01 k71 z20 z21 "
-            "l100 l101 l102 l300 l103 l010 l301 l011 l302 l012 l013 m00 l000 l303 "
-            "l001 l002 m01 l003 l310 l210 l211 l311 l212 l312 l213 l200 m10 l201 "
-            "l313 l202 l203 m11 l110 l111 l112 l113 "
-        ).split()
-        lags = {"w": (0, 1, 4, 6, 6), "y": (0, 2, 6, 7, 12), "x": (0, 1, 6, 11, 12), "k": (0, 0, 1, 8, 13), "z": (0, 4, 5, 9, 11), "l": (0, 4, 8, 9, 10), "m": (0, 8, 12, 12, 12), "K": (0, 4, 7, 8, 10), "b": (0, 0, 1, 3, 10)}
-        last = max(max(v) for v in lags.values())
-        for step in range(len(order) + last):
+        steps = len(items) + max(max(lags) for lags in LAGS.values())
+        for step in range(steps):
             for stage in (4, 3, 2, 1, 0):
-                for i, key in enumerate(order):
-                    if i + lags[key[0]][stage] == step and items[key][stage] is not None:
-                        items[key][stage]()
+                for i, (kind, stages) in enumerate(items):
+                    if i + LAGS[kind][stage] == step and stages[stage] is not None:
+                        stages[stage]()

from contextlib import ExitStack

import concourse.mybir as mybir
from concourse.masks import make_identity

M, N, E, D, HK, H, HV = 512, 1024, 1024, 1024, 8, 4, 2
FLOPS = 2 * M * E * D + 2 * N * E * D + 2 * H * M * N * D

F32 = mybir.dt.float32
BF16 = mybir.dt.bfloat16
I32 = mybir.dt.int32
U32 = mybir.dt.uint32
U8 = mybir.dt.uint8
FP8 = mybir.dt.float8_e4m3fn
FP8X4 = mybir.dt.float8_e4m3fn_x4
FP4X4 = mybir.dt.float4_e2m1fn_x4
MULT = mybir.AluOpType.mult
ADD = mybir.AluOpType.add
RELU = mybir.ActivationFunctionType.Relu
COPY = mybir.ActivationFunctionType.Copy

P = 128
PASS = 512
BANK = 512
MIXED = 3

WQ_PLANES_ON_VECTOR = (1, 0, 4, 2)
HEADS_ON_SCALAR = (1, 1, 0, 0, 0, 2, 0, 1)
MAPS_ON_SCALAR = (0, 0, 0, 1, 1, 1)

LOADS = "scale y0 heads x1 x3 y2 w1 x2 y4 x0 wk_scales y6 w0 wk w3 w2".split()
INPUT_ITEMS = "scale y1 x1 x3 heads y0 y3 w1 y2 x2 y5 x0 y4 y7 y6 wk w0 w3 w2".split()
KEY_HALVES = (0, 1)
QUERY_TILES = (1, 3, 0, 2)
GROUPS = ((1, 0), (0, 0), (2, 1), (0, 1), (2, 0), (1, 1))
QUERIES_AMONG_KEYS = (5, 1)
MIXED_AMONG_MAPS = (3, 1.5)
LAGS = {
    "scale": (0, 0, 1, 5, 5),
    "heads": (0, 1, 3, 3, 5),
    "w": (0, 4, 10, 10, 10),
    "y": (0, 3, 4, 8, 13),
    "x": (0, 0, 1, 8, 13),
    "wk": (0, 4, 5, 11, 13),
    "key": (0, 0, 3, 9, 9),
    "query": (0, 4, 5, 7, 10),
    "map": (0, 0, 2, 7, 7),
    "relu": (0, 0, 2, 7, 7),
    "mix": (0, 3, 5, 5, 11),
}


def tile_talking_heads_relu_map_s11_kernel(
    tc, x, wq, y_bytes, y_scale, wk_words, wk_scales, pl, pw, out
):
    nc = tc.nc
    with ExitStack() as ctx:
        keep = ctx.enter_context(tc.tile_pool(name="keep", bufs=1))
        work = ctx.enter_context(tc.tile_pool(name="work", bufs=3))
        psum = ctx.enter_context(tc.psum_pool(name="psum", bufs=8))
        ctx.enter_context(tc.manual_schedule())

        x_sb = keep.tile([P, 4, E], BF16, align_bytes=64)
        wq_raw = keep.tile([P, 4, 4, PASS], BF16, align_bytes=64)
        y_codes = keep.tile([P, 8, E], U8, align_bytes=64)
        scale_rows = keep.tile([P, E], F32, align_bytes=64)
        scale_cols = keep.tile([P, 2, 4], F32, align_bytes=64)
        wk_words_raw = keep.tile([P, 2, 2 * D], U8, align_bytes=64)
        wk_scales_raw = keep.tile([P, 2, D], U8, align_bytes=64)
        wk_w = keep.tile([P, 4 * D], U8, align_bytes=64)
        wk_s = keep.tile([P, 2 * D], U8, align_bytes=64)
        heads_row = keep.tile([P, H * HK + H * HV], BF16, align_bytes=64)

        nc.vector.memset(heads_row[:], 0.0)
        nc.vector.memset(wk_scales_raw[:].bitcast(I32), 0)

        def load_y(a):
            rows = y_bytes[a * P : (a + 2) * P, :]
            nc.sync.dma_start(out=y_codes[:, a : a + 2, :], in_=rows.rearrange("(a p) k -> p a k", p=P))

        def load_wq(c):
            g, e = c // 2, c % 2
            block = wq[PASS * e : PASS * (e + 1), PASS * g : PASS * (g + 1)]
            nc.sync.dma_start(out=wq_raw[:, c], in_=block.rearrange("(p j) d -> p j d", j=4))

        def load_x(mt):
            nc.sync.dma_start(out=x_sb[:, mt], in_=x[P * mt : P * (mt + 1), :])

        def load_wk():
            nc.sync.dma_start(out=wk_words_raw[:], in_=wk_words.rearrange("e p b -> p e b"))

        def load_wk_scales():
            for q in range(4):
                nc.sync.dma_start(
                    out=wk_scales_raw[32 * q : 32 * q + 4].bitcast(I32),
                    in_=wk_scales.bitcast(I32)[:, 4 * q : 4 * q + 4, :].rearrange("e s n -> s e n"),
                )

        def load_scale():
            nc.sync.dma_start(out=scale_cols[:], in_=y_scale.rearrange("o (b p m) -> p (o b) m", b=2, m=4))

        def load_heads():
            nc.sync.dma_start(out=heads_row[0:1, 0 : H * HK], in_=pl.rearrange("(o h) i -> o (h i)", o=1))
            nc.sync.dma_start(out=heads_row[0:1, H * HK :], in_=pw.rearrange("(o h) v -> o (h v)", o=1))

        loads = {"scale": load_scale, "heads": load_heads, "wk": load_wk, "wk_scales": load_wk_scales}
        for a in range(4):
            loads["w%d" % a] = lambda c=a: load_wq(c)
            loads["x%d" % a] = lambda mt=a: load_x(mt)
            loads["y%d" % (2 * a)] = lambda nt=2 * a: load_y(nt)
        for name in LOADS:
            loads[name]()

        ident = keep.tile([P, P], F32)
        make_identity(nc, ident[:])
        ones = keep.tile([P, P], BF16)
        nc.gpsimd.memset(ones[:], 1.0)
        pl_col = keep.tile([P, H, 2], F32)
        pw_row = keep.tile([P, H * HV], F32)
        pw_col = keep.tile([P, HV], F32)
        fold = keep.tile([P, 32], F32)
        mixer = keep.tile([P, 2, P], F32)
        nc.gpsimd.tensor_tensor(out=fold[:], in0=ident[:, 0:32], in1=ident[:, 32:64], op=ADD)
        nc.gpsimd.tensor_tensor(out=fold[:], in0=fold[:], in1=ident[:, 64:96], op=ADD)
        nc.gpsimd.tensor_tensor(out=fold[:], in0=fold[:], in1=ident[:, 96:128], op=ADD)
        nc.gpsimd.memset(mixer[:], 0.0)

        x_c = keep.tile([P, 4, 256], U32, align_bytes=64)
        x_s = keep.tile([P, 4, 256], U8, align_bytes=64)
        y_c = keep.tile([P, 8, 256], U32, align_bytes=64)
        y_s = keep.tile([P, 8, 256], U8, align_bytes=64)
        wq_c = keep.tile([P, 4, PASS], U32, align_bytes=64)
        wq_s = keep.tile([P, 4, PASS], U8, align_bytes=64)
        key_c = keep.tile([P, 4, BANK], U32, align_bytes=64)
        key_s = keep.tile([P, 4, BANK], U8, align_bytes=64)
        z_c = keep.tile([P, 8, H * P], U32, align_bytes=64)
        z_s = keep.tile([P, 8, H * P], U8, align_bytes=64)

        def bank(name):
            return psum.tile([P, BANK], F32, tag="bank", name=name)

        def scale_item():
            s = {}

            def tensor():
                for b in range(2):
                    s[b] = bank("scale%d" % b)
                    for m in range(4):
                        column = scale_cols[:, b, m : m + 1].to_broadcast([P, P])
                        nc.tensor.transpose(s[b][:, P * m : P * (m + 1)], column, ident[:])

            def empty():
                for b in range(2):
                    row = scale_rows[:, PASS * b : PASS * (b + 1)]
                    nc.scalar.copy(
                        out=row.rearrange("p (i m) -> p i m", m=4), in_=s[b][:].rearrange("p (m i) -> p i m", m=4)
                    )

            return (None, tensor, empty, None, None)

        def heads_item():
            s = {}

            def tensor():
                s["all"] = bank("heads")
                nc.tensor.matmul(s["all"][:, 0 : H * HK + H * HV], lhsT=ones[:], rhs=heads_row[:], start=True, stop=True)

            def empty():
                pl_all = s["all"][:, 0 : H * HK].rearrange("p (h g q) -> p h g q", h=H, g=2)
                pw_all = s["all"][:, H * HK : H * HK + H * HV]
                nc.scalar.copy(out=pw_row[:], in_=pw_all)
                for q in range(4):
                    rows = slice(32 * q, 32 * q + 32)
                    nc.scalar.copy(out=pl_col[rows], in_=pl_all[rows, :, :, q])
                    nc.scalar.copy(out=pw_col[rows], in_=pw_all[rows, HV * q : HV * (q + 1)])
                for j in range(2):
                    for v in range(HV):
                        cols = slice(64 * v + 32 * j, 64 * v + 32 * j + 32)
                        nc.gpsimd.tensor_scalar(
                            out=mixer[:, j, cols], in0=fold[:], scalar1=pw_col[:, v : v + 1], scalar2=None, op0=MULT
                        )

            return (None, tensor, empty, None, None)

        def wq_item(c):
            s = {}

            def prepare():
                s["grouped"] = work.tile([P, 4 * PASS], BF16, align_bytes=64, tag="wq", name="wq_%d" % c)
                dst = s["grouped"][:].rearrange("p (t q r j) -> p t q r j", t=4, r=8, j=4)
                src = wq_raw[:, c].rearrange("p j (q t r) -> p t q r j", t=4, r=8)
                on_vector = WQ_PLANES_ON_VECTOR[c]
                if on_vector:
                    nc.vector.tensor_copy(out=dst[:, 0:on_vector], in_=src[:, 0:on_vector])
                for t in range(on_vector, 4):
                    nc.scalar.copy(out=dst[:, t], in_=src[:, t])

            def finish():
                nc.vector.quantize_mx(out=wq_c[:, c].bitcast(FP8X4), scales=wq_s[:, c], in_=s["grouped"][:])

            return (prepare, None, None, finish, None)

        def turn(src, name):
            words = src.bitcast(F32)
            turned = bank(name)
            for e in range(2):
                for u in range(2):
                    c0 = P * (2 * e + u)
                    nc.tensor.transpose(turned[:, c0 : c0 + P], words[:, 256 * e + u : 256 * (e + 1) : 2], ident[:])
            return turned

        def empty_turned(turned, dst):
            nc.scalar.copy(
                out=dst.bitcast(F32).rearrange("p (e r u) -> p e r u", e=2, u=2),
                in_=turned[:].rearrange("p (e u r) -> p e r u", e=2, u=2),
            )

        def x_item(mt):
            s = {}

            def tensor():
                s["turned"] = turn(x_sb[:, mt, :], "turn_x%d" % mt)

            def empty():
                s["grouped"] = work.tile([P, E], BF16, align_bytes=64, tag="x", name="x_%d" % mt, bufs=2)
                empty_turned(s["turned"], s["grouped"][:])

            def finish():
                nc.vector.quantize_mx(out=x_c[:, mt].bitcast(FP8X4), scales=x_s[:, mt], in_=s["grouped"][:])

            return (None, tensor, empty, finish, None)

        def y_item(nt):
            s = {}

            def prepare():
                s["rows"] = work.tile([P, E], BF16, align_bytes=64, tag="y_rows", name="y_rows_%d" % nt)
                for b in range(2):
                    cols = slice(PASS * b, PASS * (b + 1))
                    nc.vector.tensor_tensor(
                        out=s["rows"][:, cols],
                        in0=y_codes[:, nt, cols].bitcast(FP8),
                        in1=scale_rows[:, cols],
                        op=MULT,
                    )

            def tensor():
                s["turned"] = turn(s["rows"][:], "turn_y%d" % nt)

            def empty():
                s["grouped"] = work.tile([P, E], BF16, align_bytes=64, tag="y", name="y_%d" % nt, bufs=5)
                empty_turned(s["turned"], s["grouped"][:])

            def finish():
                nc.vector.quantize_mx(out=y_c[:, nt].bitcast(FP8X4), scales=y_s[:, nt], in_=s["grouped"][:])

            return (prepare, tensor, empty, finish, None)

        def wk_item():
            def prepare():
                for dst, src, run in ((wk_w, wk_words_raw, 4), (wk_s, wk_scales_raw, 2)):
                    nc.vector.tensor_copy(
                        out=dst[:].bitcast(I32).rearrange("p (t x r) -> p t x r", t=4, r=run),
                        in_=src[:].rearrange("p e b -> p (e b)").bitcast(I32).rearrange("p (x t r) -> p t x r", t=4, r=run),
                    )

            return (prepare, None, None, None, None)

        key_grouped = {}

        def key_item(nt, g):
            s = {}
            half, a = nt // 4, nt % 4

            def tensor():
                s["key"] = bank("key%d%d" % (nt, g))
                for t in range(4):
                    for e in range(2):
                        col = P * ((2 * t + e) * 2 + g)
                        nc.tensor.matmul_mx(
                            out=s["key"][:, P * t : P * (t + 1)],
                            lhsT=wk_w[:, 2 * col : 2 * (col + P)].bitcast(FP4X4),
                            lhsT_scale=wk_s[:, col : col + P],
                            rhs=y_c[:, nt, P * e : P * (e + 1)].bitcast(FP8X4),
                            rhs_scale=y_s[:, nt, P * e : P * (e + 1)],
                            start=(e == 0),
                            stop=(e == 1),
                        )

            def empty():
                if a == 0:
                    key_grouped[half, g] = work.tile(
                        [P, 4, 4 * P], BF16, align_bytes=64, tag="key", name="key_%d%d" % (half, g), bufs=4
                    )
                nc.scalar.copy(
                    out=key_grouped[half, g][:, a, :].rearrange("p (n t) -> p n t", t=4),
                    in_=s["key"][:].rearrange("p (t n) -> p n t", t=4),
                )

            def finish():
                nc.vector.quantize_mx(
                    out=key_c[:, 2 * half + g].bitcast(FP8X4),
                    scales=key_s[:, 2 * half + g],
                    in_=key_grouped[half, g][:].rearrange("p a c -> p (a c)"),
                )

            return (None, tensor, empty, finish if a == 3 else None, None)

        def z_columns(z, mt):
            if mt == MIXED:
                return z.rearrange("p (b h c) -> p h b c", b=4, h=H)
            return z.rearrange("p (h b c) -> p h b c", h=H, b=1)

        def query_item(mt, g):
            s = {}

            def tensor():
                s["query"] = bank("query%d%d" % (mt, g))
                for t in range(4):
                    for e in range(2):
                        c = 2 * g + e
                        nc.tensor.matmul_mx(
                            out=s["query"][:, P * t : P * (t + 1)],
                            lhsT=wq_c[:, c, P * t : P * (t + 1)].bitcast(FP8X4),
                            lhsT_scale=wq_s[:, c, P * t : P * (t + 1)],
                            rhs=x_c[:, mt, P * e : P * (e + 1)].bitcast(FP8X4),
                            rhs_scale=x_s[:, mt, P * e : P * (e + 1)],
                            start=(e == 0),
                            stop=(e == 1),
                        )

            def empty():
                s["float"] = work.tile([P, BANK], F32, align_bytes=64, tag="query", name="query_%d%d" % (mt, g))
                by_token = s["query"][:].rearrange("p (t m) -> p m t", t=4)
                nc.scalar.copy(out=s["float"][:].rearrange("p (m t) -> p m t", t=4), in_=by_token)
                s["z"] = work.tile([P, H * BANK], BF16, align_bytes=64, tag="z", name="z_%d%d" % (mt, g), bufs=4)
                for h in range(HEADS_ON_SCALAR[2 * mt + g]):
                    dst = z_columns(s["z"][:], mt)[:, h].rearrange("p b (m t) -> p b m t", t=4)
                    nc.scalar.activation(
                        out=dst,
                        in_=by_token.rearrange("p (b m) t -> p b m t", b=dst.shape[1]),
                        func=COPY,
                        scale=pl_col[:, h, g : g + 1],
                    )

            def finish():
                for h in range(HEADS_ON_SCALAR[2 * mt + g], H):
                    dst = z_columns(s["z"][:], mt)[:, h]
                    nc.vector.tensor_scalar(
                        out=dst,
                        in0=s["float"][:].rearrange("p (b c) -> p b c", b=dst.shape[1]),
                        scalar1=pl_col[:, h, g : g + 1],
                        scalar2=None,
                        op0=MULT,
                    )

            def finish_further():
                nc.vector.quantize_mx(out=z_c[:, 2 * mt + g].bitcast(FP8X4), scales=z_s[:, 2 * mt + g], in_=s["z"][:])

            return (None, tensor, empty, finish, finish_further)

        def logits(mt, half, block):
            result = bank("logits%d%d%d" % (mt, half, block))
            cols = slice(P * block, P * (block + 1))
            for g in range(2):
                nc.tensor.matmul_mx(
                    out=result[:],
                    lhsT=z_c[:, 2 * mt + g, cols].bitcast(FP8X4),
                    lhsT_scale=z_s[:, 2 * mt + g, cols],
                    rhs=key_c[:, 2 * half + g].bitcast(FP8X4),
                    rhs_scale=key_s[:, 2 * half + g],
                    start=(g == 0),
                    stop=(g == 1),
                )
            return result

        sums = {}

        def map_item(mt, half, h):
            s = {}
            on_scalar = MAPS_ON_SCALAR[3 * half + mt]

            def tensor():
                s["logits"] = logits(mt, half, h)

            def empty():
                s["att"] = work.tile([P, BANK], F32, tag="att", name="att%d%d%d" % (mt, half, h), bufs=8)
                nc.scalar.activation(out=s["att"][:], in_=s["logits"][:], func=RELU)
                if h == 0:
                    for v in range(HV):
                        sums[mt, half, v] = work.tile(
                            [P, BANK], F32, tag="sum%d" % v, name="sum%d%d%d" % (mt, half, v), bufs=3
                        )
                        if v < on_scalar:
                            nc.scalar.activation(
                                out=sums[mt, half, v][:], in_=s["att"][:], func=COPY, scale=pw_row[:, v : v + 1]
                            )

            def finish():
                for v in range(HV):
                    weight = pw_row[:, HV * h + v : HV * h + v + 1]
                    total = sums[mt, half, v]
                    if h > 0:
                        nc.vector.scalar_tensor_tensor(
                            out=total[:], in0=s["att"][:], scalar=weight, in1=total[:], op0=MULT, op1=ADD
                        )
                    elif v >= on_scalar:
                        nc.vector.tensor_scalar(out=total[:], in0=s["att"][:], scalar1=weight, scalar2=None, op0=MULT)
                    if h == H - 1:
                        nc.sync.dma_start(
                            out=out[v, P * mt : P * (mt + 1), BANK * half : BANK * (half + 1)], in_=total[:]
                        )

            return (None, tensor, empty, finish, None)

        atts = {}

        def relu_item(half, block):
            s = {}

            def tensor():
                s["logits"] = logits(MIXED, half, block)

            def empty():
                atts[half, block] = work.tile([P, BANK], F32, tag="relu", name="relu%d%d" % (half, block), bufs=4)
                nc.scalar.activation(out=atts[half, block][:], in_=s["logits"][:], func=RELU)

            return (None, tensor, empty, None, None)

        def mix_item(half, pair):
            s = {}

            def tensor():
                s["mix"] = bank("mix%d%d" % (half, pair))
                for j in range(2):
                    nc.tensor.matmul(
                        s["mix"][:],
                        lhsT=mixer[:, j, :],
                        rhs=atts[half, 2 * pair + j][:],
                        start=(j == 0),
                        stop=(j == 1),
                    )

            def empty():
                res = work.tile([P, BANK], F32, tag="res", name="res%d%d" % (half, pair), bufs=2)
                nc.scalar.copy(out=res[:], in_=s["mix"][:])
                m0 = P * MIXED + 64 * pair
                for v in range(HV):
                    nc.sync.dma_start(
                        out=out[v, m0 : m0 + 64, BANK * half : BANK * (half + 1)], in_=res[64 * v : 64 * (v + 1), :]
                    )

            return (None, tensor, empty, None, None)

        items = []
        for name in INPUT_ITEMS:
            if name == "scale":
                items.append((name, scale_item()))
            elif name == "heads":
                items.append((name, heads_item()))
            elif name == "wk":
                items.append((name, wk_item()))
            else:
                kind, number = name[0], int(name[1])
                items.append((kind, {"w": wq_item, "y": y_item, "x": x_item}[kind](number)))

        keys = [("key", key_item(4 * half + a, g)) for half in KEY_HALVES for g in range(2) for a in range(4)]
        queries = [("query", query_item(mt, g)) for mt in QUERY_TILES for g in range(2)]
        maps = [("map", map_item(mt, half, h)) for mt, half in GROUPS for h in range(H)]
        mixed = []
        for half in range(2):
            relus = [("relu", relu_item(half, block)) for block in range(4)]
            mixes = [("mix", mix_item(half, pair)) for pair in range(2)]
            mixed += relus[0:3] + mixes[0:1] + relus[3:4] + mixes[1:2]

        def weave(main, side, first, every):
            woven, taken = [], 0
            for i, item in enumerate(main):
                woven.append(item)
                while taken < len(side) and i >= first + every * taken:
                    woven.append(side[taken])
                    taken += 1
            return woven + side[taken:]

        items += weave(keys, queries, *QUERIES_AMONG_KEYS)
        items += weave(maps, mixed, *MIXED_AMONG_MAPS)

        steps = len(items) + max(max(lags) for lags in LAGS.values())
        for step in range(steps):
            for stage in (4, 3, 2, 1, 0):
                for i, (kind, stages) in enumerate(items):
                    if i + LAGS[kind][stage] == step and stages[stage] is not None:
                        stages[stage]()
